import numpy as np
import ml_dtypes

BF16 = ml_dtypes.bfloat16


def bf(x):
    return np.asarray(x, np.float32).astype(BF16)


def f32(x):
    return np.asarray(x, np.float32)


def f64(x):
    return np.asarray(x).astype(np.float64)


def striped(idx):
    return np.tile(idx.reshape(-1, 16).T, (8, 1))


S, K, N, E, Q, H, O = 256, 512, 256, 2, 128, 128, 128


def setup_inputs():
    return {"table": bf(np.random.standard_normal((K, S))), "w": bf(np.random.standard_normal((E, K, H)) / np.sqrt(K)), "b": f32(0.5 * np.random.standard_normal((H, E))), "w2": bf(np.random.standard_normal((E, H, O)) / np.sqrt(H)), "c": f32(0.2 + 0.8 * np.random.random_sample((1, N))), "offs": striped(np.sort(np.random.permutation(S).reshape(E, Q), axis=1).reshape(-1))}


def reference(table, w, b, w2, c, offs):
    idx = offs[:16].T.reshape(-1)
    x = f64(table)[:, idx]
    ys = []
    for e in range(E):
        t = f64(w)[e].T @ x[:, e * Q : (e + 1) * Q] + f64(b)[:, e : e + 1]
        t = np.maximum(t, 0.0)
        ys.append(f64(w2)[e].T @ t)
    return np.concatenate(ys, axis=1) * f64(c)

@@ -1,0 +1,67 @@
+import concourse.mybir as mybir
+
+P = 128
+TOKENS = 256
+FEATURES = 512
+EXPERTS = 2
+PIECE = TOKENS // EXPERTS
+HIDDEN = 128
+OUT_FEATURES = 128
+PAIR = 2
+HALVES = FEATURES // (P * PAIR)
+LIST_COLUMNS = PIECE // 16
+
+FLOPS = 2 * TOKENS * (FEATURES * HIDDEN + HIDDEN * OUT_FEATURES)
+
+BF16, F32, U16 = mybir.dt.bfloat16, mybir.dt.float32, mybir.dt.uint16
+ALU = mybir.AluOpType
+
+
+def tile_rows_ffn2_relu_kernel(tc, table, w, b, w2, c, offs, out):
+    nc = tc.nc
+    table_halves = table.rearrange("(half p a) s -> half p a s", half=HALVES, a=PAIR)
+    w_halves = w.rearrange("e (half p a) i -> half p e a i", half=HALVES, a=PAIR)
+
+    with (
+        tc.tile_pool(name="held", bufs=1) as held,
+        tc.psum_pool(name="psum", bufs=1) as psum,
+    ):
+        offsets = held.tile([P, TOKENS // 16], U16, name="offsets")
+        tokens = [held.tile([P, PAIR, TOKENS], BF16, name=f"tokens{half}") for half in range(HALVES)]
+        first_w = [held.tile([P, EXPERTS, PAIR, HIDDEN], BF16, name=f"first_w{half}") for half in range(HALVES)]
+        bias = held.tile([P, EXPERTS], F32, name="bias")
+        second_w = held.tile([P, EXPERTS, OUT_FEATURES], BF16, name="second_w")
+        router = held.tile([P, TOKENS], F32, name="router")
+
+        nc.sync.dma_start(offsets[:], offs)
+        for half in range(HALVES):
+            nc.sync.dma_start(tokens[half][:], table_halves[half])
+            nc.scalar.dma_start(first_w[half][:], w_halves[half])
+        nc.scalar.dma_start(bias[:], b)
+        nc.scalar.dma_start(second_w[:], w2.rearrange("e i o -> i e o"))
+        nc.sync.dma_start(router[:], c[0].partition_broadcast(P))
+
+        pre = [psum.tile([P, PIECE], F32, name=f"pre{e}") for e in range(EXPERTS)]
+        for half in range(HALVES):
+            for e in range(EXPERTS):
+                piece = offsets[:, e * LIST_COLUMNS : (e + 1) * LIST_COLUMNS]
+                for a in range(PAIR):
+                    nc.tensor.matmul(
+                        pre[e][:],
+                        first_w[half][:, e, a, :],
+                        tokens[half][:, a, :].indirect(piece),
+                        start=(half == 0 and a == 0),
+                        stop=(half == HALVES - 1 and a == PAIR - 1),
+                    )
+
+        hidden = held.tile([P, EXPERTS, PIECE], BF16, name="hidden")
+        for e in range(EXPERTS):
+            nc.vector.tensor_scalar(hidden[:, e, :], pre[e][:], bias[:, e : e + 1], 0.0, ALU.add, ALU.max)
+
+        result = held.tile([P, TOKENS], F32, name="result")
+        for e in range(EXPERTS):
+            columns = slice(e * PIECE, (e + 1) * PIECE)
+            post = psum.tile([P, PIECE], F32, name=f"post{e}")
+            nc.tensor.matmul(post[:], second_w[:, e, :], hidden[:, e, :], start=True, stop=True)
+            nc.vector.tensor_tensor(result[:, columns], post[:], router[:, columns], ALU.mult)
+        nc.sync.dma_start(out, result[:])

@@ -31,15 +31,22 @@ def tile_rows_ffn2_relu_kernel(tc, table, w, b, w2, c, offs, out):
         first_w = [held.tile([P, EXPERTS, PAIR, HIDDEN], BF16, name=f"first_w{half}") for half in range(HALVES)]
         bias = held.tile([P, EXPERTS], F32, name="bias")
         second_w = held.tile([P, EXPERTS, OUT_FEATURES], BF16, name="second_w")
+        router_row = held.tile([1, TOKENS], F32, name="router_row")
+        ones = held.tile([1, P], F32, name="ones")
         router = held.tile([P, TOKENS], F32, name="router")
 
         nc.sync.dma_start(offsets[:], offs)
+        nc.scalar.dma_start(router_row[:], c)
         for half in range(HALVES):
             nc.sync.dma_start(tokens[half][:], table_halves[half])
             nc.scalar.dma_start(first_w[half][:], w_halves[half])
         nc.scalar.dma_start(bias[:], b)
         nc.scalar.dma_start(second_w[:], w2.rearrange("e i o -> i e o"))
-        nc.sync.dma_start(router[:], c[0].partition_broadcast(P))
+
+        nc.vector.memset(ones[:], 1.0)
+        spread = psum.tile([P, TOKENS], F32, name="spread")
+        nc.tensor.matmul(spread[:], ones[:], router_row[:], start=True, stop=True)
+        nc.vector.tensor_copy(router[:], spread[:])
 
         pre = [psum.tile([P, PIECE], F32, name=f"pre{e}") for e in range(EXPERTS)]
         for half in range(HALVES):

import concourse.mybir as mybir

P = 128
TOKENS = 256
FEATURES = 512
EXPERTS = 2
PIECE = TOKENS // EXPERTS
HIDDEN = 128
OUT_FEATURES = 128
PAIR = 2
HALVES = FEATURES // (P * PAIR)
LIST_COLUMNS = PIECE // 16

FLOPS = 2 * TOKENS * (FEATURES * HIDDEN + HIDDEN * OUT_FEATURES)

BF16, F32, U16 = mybir.dt.bfloat16, mybir.dt.float32, mybir.dt.uint16
ALU = mybir.AluOpType


def tile_rows_ffn2_relu_kernel(tc, table, w, b, w2, c, offs, out):
    nc = tc.nc
    table_halves = table.rearrange("(half p a) s -> half p a s", half=HALVES, a=PAIR)
    w_halves = w.rearrange("e (half p a) i -> half p e a i", half=HALVES, a=PAIR)

    with (
        tc.tile_pool(name="held", bufs=1) as held,
        tc.psum_pool(name="psum", bufs=1) as psum,
    ):
        offsets = held.tile([P, TOKENS // 16], U16, name="offsets")
        tokens = [held.tile([P, PAIR, TOKENS], BF16, name=f"tokens{half}") for half in range(HALVES)]
        first_w = [held.tile([P, EXPERTS, PAIR, HIDDEN], BF16, name=f"first_w{half}") for half in range(HALVES)]
        bias = held.tile([P, EXPERTS], F32, name="bias")
        second_w = held.tile([P, EXPERTS, OUT_FEATURES], BF16, name="second_w")
        router_row = held.tile([1, TOKENS], F32, name="router_row")
        ones = held.tile([1, P], F32, name="ones")
        router = held.tile([P, TOKENS], F32, name="router")

        nc.sync.dma_start(offsets[:], offs)
        nc.scalar.dma_start(router_row[:], c)
        for half in range(HALVES):
            nc.sync.dma_start(tokens[half][:], table_halves[half])
            nc.scalar.dma_start(first_w[half][:], w_halves[half])
        nc.scalar.dma_start(bias[:], b)
        nc.scalar.dma_start(second_w[:], w2.rearrange("e i o -> i e o"))

        nc.vector.memset(ones[:], 1.0)
        spread = psum.tile([P, TOKENS], F32, name="spread")
        nc.tensor.matmul(spread[:], ones[:], router_row[:], start=True, stop=True)
        nc.vector.tensor_copy(router[:], spread[:])

        pre = [psum.tile([P, PIECE], F32, name=f"pre{e}") for e in range(EXPERTS)]
        for half in range(HALVES):
            for e in range(EXPERTS):
                piece = offsets[:, e * LIST_COLUMNS : (e + 1) * LIST_COLUMNS]
                for a in range(PAIR):
                    nc.tensor.matmul(
                        pre[e][:],
                        first_w[half][:, e, a, :],
                        tokens[half][:, a, :].indirect(piece),
                        start=(half == 0 and a == 0),
                        stop=(half == HALVES - 1 and a == PAIR - 1),
                    )

        hidden = held.tile([P, EXPERTS, PIECE], BF16, name="hidden")
        for e in range(EXPERTS):
            nc.vector.tensor_scalar(hidden[:, e, :], pre[e][:], bias[:, e : e + 1], 0.0, ALU.add, ALU.max)

        result = held.tile([P, TOKENS], F32, name="result")
        for e in range(EXPERTS):
            columns = slice(e * PIECE, (e + 1) * PIECE)
            post = psum.tile([P, PIECE], F32, name=f"post{e}")
            nc.tensor.matmul(post[:], second_w[:, e, :], hidden[:, e, :], start=True, stop=True)
            nc.vector.tensor_tensor(result[:, columns], post[:], router[:, columns], ALU.mult)
        nc.sync.dma_start(out, result[:])
